import numpy as np, ml_dtypes
CORES = [51,54,179,182]
N = 4
import mx_ref
BF = ml_dtypes.bfloat16
def entries(a):
    return np.ascontiguousarray(a.T).reshape(-1)
def table(e):
    return np.ascontiguousarray(np.reshape(e, (-1, 16)).T).astype(np.int32)
def cut(t, i, w=512):
    return t[:, w * i:w * i + w]
def f(rng, *shape):
    return mx_ref.flush((rng.standard_normal(shape, dtype=np.float32) * np.exp2(rng.integers(-2, 3, shape[:-1] + (1,)))).astype(BF))
def wide(rng, *shape, cols=0):
    v = rng.standard_normal(shape, dtype=np.float32) * np.exp2(rng.integers(-12, 13, shape)).astype(np.float32)
    if cols: v *= np.repeat(np.exp2(rng.integers(-cols, cols + 1, shape[:-2] + (1, shape[-1] // 4))) * (rng.random(shape[:-2] + (1, shape[-1] // 4)) > 0.0625), 4, axis=-1).astype(np.float32)
    return mx_ref.flush(v.astype(BF))
PG, NW, SP, CW, CP, O = 24, 64, 32, 32, 12, 2
def counts(rng, total, cap, least):
    n = np.array(least)
    while n.sum() < total: n[rng.choice(np.flatnonzero(n < cap))] += 1
    return n
def lists(rng, full=False, own=False, shared=False, rewritten=False):
    h = int(rng.integers(0, N)); hot = rng.permutation(PG)[:CP if shared else 2]
    fr, pg = np.zeros((N, SP), int), np.zeros((N, SP), int)
    rd, wr, wp = np.full((N, N * CP), -1), np.full((N, N * CW), -1), np.full((N, N * CW), -1)
    for s in range(N):
        lw, lp = np.zeros(N, int), np.zeros(N, int)
        if full:
            a = np.append(h, rng.permutation(np.delete(np.arange(N), h)))
            lw[a[:NW // CW]] = CW; lp[a[:SP // CP]] = CP
        if own: lw[s] = CW; lp[s] = CP
        if shared: lw[h] = CW; lp[h] = CP
        if rewritten: lw[h] = CW; lp[h] = 1
        n, fresh, at = counts(rng, NW, CW, lw), rng.permutation(NW), 0
        for q in range(N):
            c = rng.permutation(CW)[:n[q]]
            wr[s, q * CW + c] = fresh[at:at + n[q]]; wp[q, s * CW + c] = 0; at += n[q]
        n, slots, frames = counts(rng, SP, CP, lp), [], []
        for q in range(N):
            must = np.zeros(0, int)
            if q == h and shared: must = hot
            if q == h and rewritten: must = hot[s % 2:s % 2 + 1]
            g = np.concatenate([must, rng.permutation(np.setdiff1d(np.arange(PG), must))])[:n[q]]
            c = rng.permutation(CP)[:n[q]]
            rd[q, s * CP + c] = g; slots.append(q * CP + c); frames.append(q * PG + g)
        o = rng.permutation(SP)
        pg[s] = np.concatenate(slots)[o]; fr[s] = np.concatenate(frames)[o]
    for q in range(N):
        k = np.flatnonzero(wp[q] >= 0); must = np.zeros(0, int)
        if q == h and shared: must = 16 * hot + rng.integers(0, 16, hot.size)
        if q == h and rewritten: must = (16 * hot[:, None] + np.arange(16)).reshape(-1)
        p = np.concatenate([must, rng.permutation(np.setdiff1d(np.arange(16 * PG), must))])[:k.size]
        wp[q, k] = rng.permutation(p)
    return {n: np.stack([table(v) for v in a]) for n, a in (("fr", fr), ("wr", wr), ("wp", wp), ("rd", rd), ("pg", pg))}
def setup_inputs(rng):
    return {"pl": f(rng, N, 128, 64 * PG), "nw": f(rng, N, 128, 4 * NW), "qw": f(rng, N, 128, 512 * O), **lists(rng)}
def setup_inputs_full(rng):
    return {**setup_inputs(rng), **lists(rng, full=True)}
def setup_inputs_own(rng):
    return {**setup_inputs(rng), **lists(rng, own=True)}
def setup_inputs_rewritten(rng):
    return {**setup_inputs(rng), **lists(rng, rewritten=True)}
def setup_inputs_shared(rng):
    return {**setup_inputs(rng), **lists(rng, shared=True)}
def setup_inputs_spread(rng):
    d = setup_inputs(rng); d["pl"] = wide(rng, N, 128, 64 * PG, cols=8); d["nw"] = wide(rng, N, 128, 4 * NW, cols=8); return d
def check_inputs(d):
    b = []
    for r in range(N):
        t, a, p, k, g = [entries(d[n][r]) for n in ("fr", "wr", "wp", "rd", "pg")]
        if t.min() < 0 or t.max() >= N * PG or len(set(t.tolist())) != SP: b.append("fr")
        if a.min() < -1 or a.max() >= NW or sorted(a[a >= 0].tolist()) != list(range(NW)): b.append("wr")
        sent = np.concatenate([entries(d["wr"][s])[r * CW:r * CW + CW] for s in range(N)]); v = p[p >= 0]
        if p.min() < -1 or p.max() >= 16 * PG or len(set(v.tolist())) != v.size or ((p >= 0) != (sent >= 0)).any(): b.append("wp")
        if k.min() < -1 or k.max() >= PG: b.append("rd")
        got = np.concatenate([entries(d["rd"][q])[r * CP:r * CP + CP] for q in range(N)])
        if g.min() < 0 or g.max() >= N * CP or len(set(g.tolist())) != SP or (got >= 0).sum() != SP: b.append("pg")
        elif (got[g] < 0).any() or (g // CP * PG + got[g] != t).any(): b.append("pg")
    return b
def reference(pl, nw, qw, fr, wr, wp, rd, pg):
    pools = []
    for q in range(N):
        v = pl[q].reshape(128, 16 * PG, 4).copy()
        for s in range(N):
            c, p = entries(wr[s])[q * CW:q * CW + CW], entries(wp[q])[s * CW:s * CW + CW]
            k = p >= 0
            v[:, p[k]] = nw[s].reshape(128, NW, 4)[:, c[k]]
        pools.append(v)
    pools = np.concatenate(pools, axis=1)
    y = np.zeros((N, 128, O * SP * 16), np.float32)
    for r in range(N):
        e = (16 * entries(fr[r])[:, None] + np.arange(16)).reshape(-1)
        pages = mx_ref.quantize(np.ascontiguousarray(pools[:, e]).reshape(128, -1))
        for o in range(O):
            y[r][:, SP * 16 * o:SP * 16 * o + SP * 16] = mx_ref.matmul(mx_ref.quantize(np.ascontiguousarray(cut(qw[r], o))), pages)
    return {"y": y}

@@ -1,0 +1,222 @@
+from concourse.bass import DstId, RemoteDMATransfer
+from concourse.mybir import dt, AluOpType, ActivationFunctionType
+
+N, PG, NW, SP, CW, CP, O = 4, 24, 64, 32, 32, 12, 2
+NSL = N * CW
+PC = 16 * CP
+F8, U8 = "float8_e4m3fn_x4", "uint8"
+SCRATCH = {
+    "nwt": ("sbuf", [128, 512], "bfloat16"), "plt": ("sbuf", [128, 64 * PG], "bfloat16"), "qwt": ("sbuf", [128, 512 * O], "bfloat16"),
+    "nwq": ("sbuf", [128, 128], F8), "nws": ("sbuf", [128, 128], U8),
+    "sl1": ("sbuf", [128, NSL], F8), "sl1s": ("sbuf", [128, NSL], U8),
+    "win": ("sbuf", [128, NSL + 16 * PG], F8), "wins": ("sbuf", [128, NSL + 16 * PG], U8),
+    "sl2": ("sbuf", [128, N * PC], F8), "sl2s": ("sbuf", [128, N * PC], U8),
+    "land": ("sbuf", [128, N * PC], F8), "lands": ("sbuf", [128, N * PC], U8),
+    "qwq": ("sbuf", [128, 128 * O], F8), "qws": ("sbuf", [128, 128 * O], U8),
+    "wr32": ("sbuf", [128, 8], "int32"), "wp32": ("sbuf", [128, 8], "int32"),
+    "rd32": ("sbuf", [128, 3], "int32"), "pg32": ("sbuf", [128, 2], "int32"),
+    "o1": ("sbuf", [128, 8], "uint16"), "o2": ("sbuf", [128, 8], "uint16"), "rdo": ("sbuf", [128, 4], "uint16"),
+    "o3": ("sbuf", [128, 48], "uint16"), "pgo": ("sbuf", [128, 2], "uint16"), "o4": ("sbuf", [128, 32], "uint16"),
+    "pi": ("sbuf", [128, 1], "int32"), "pb": ("sbuf", [128, 4], "int32"), "col": ("sbuf", [128, 4], "float32"),
+    "kv": ("sbuf", [128, NSL], "bfloat16"), "ki": ("sbuf", [128, 8], "int32"), "kk": ("sbuf", [128, 8], "int32"),
+    "bi": ("sbuf", [128, 25], "int32"), "be": ("sbuf", [128, 25], "float32"),
+    "si": ("sbuf", [128, 48], "int32"), "se": ("sbuf", [128, 48], "float32"),
+    "t1": ("sbuf", [128, 8], "int32"), "t2": ("sbuf", [128, 8], "int32"),
+    "X": ("sbuf", [128, 528], "bfloat16"), "TX": ("sbuf", [128, 416], "bfloat16"), "wc": ("sbuf", [128, 25], "float32"),
+    "ps": ("psum", [128, 512 * N * O], "float32"),
+    "r0": ("sbuf", [128, N * PC], "float32"), "r1": ("sbuf", [128, N * PC], "float32"),
+    "y0": ("sbuf", [128, 512], "float32"), "y1": ("sbuf", [128, 512], "float32"),
+}
+SEMAPHORES = (["l_nw", "l_wr", "l_wp", "l_rd", "l_pg", "l_pl", "l_qw", "stored"]
+              + ["io_c", "c_nw", "c_x", "c_b", "c_c", "c_d", "q_nw", "q_pl", "q_qw", "v_o1", "v_t1", "v_t2", "v_o2", "v_x", "v_tx",
+                 "v_wc", "v_rdo", "v_o3", "v_pgo", "v_o4"]
+              + ["p1c", "p1s", "own1c", "own1s", "a1c", "a1s", "sent1", "sent2"]
+              + [n + str(r) for n in ("p2c", "p2s", "a2c", "a2s", "m0_", "m1_", "k0_", "k1_") for r in range(N)]
+              + ["f0v", "f0s", "f1v", "f1s"])
+
+
+def plan(src, cores, topo):
+    others = [c for c in cores if c != src]
+    off = [c for c in others if c not in topo.cores_of(src)]
+    off.sort(key=lambda c: topo.die(c) == topo.die(src))
+    near = [c for c in others if c not in off]
+    out_eng = topo.engines(src, off[0])
+    k = len(off)
+    p = [(c, True, out_eng[j::k], out_eng) for j, c in enumerate(off)]
+    for c in near:
+        e = [x for x in topo.engines(src, c) if x not in out_eng]
+        p.append((c, False, e[::2], e))
+    return p
+
+
+def mask_of(engines):
+    return sum(1 << e for e in engines)
+
+
+def rank_program(g, core, T, topo):
+    me = T.rank_of(core)
+    if me is None:
+        return
+    V, S, P, Y, sem = g.vector, g.scalar, g.tensor, g.sync, T.sem
+    A, COPY = AluOpType, ActivationFunctionType.Copy
+    my = plan(core, T.cores, topo)
+    dests = [T.rank_of(c) for c, _, _, _ in my]
+    where = {T.rank_of(c): topo.addr(c, core) for c, _, _, _ in my}
+    e1 = {T.rank_of(c): e for c, _, e, _ in my}
+    e2 = {T.rank_of(c): e for c, _, _, e in my}
+    from1, from2 = {}, {}
+    for s in range(N):
+        if s != me:
+            for c, _, a, b in plan(T.cores[s], T.cores, topo):
+                if c == core:
+                    from1[s], from2[s] = len(a), len(b)
+
+    def send(out, in_, d, engines, arrive):
+        rid, pid = where[d]
+        return RemoteDMATransfer(dst_ids=[DstId(rid=rid, pnc=pid)], dma_engine_mask=mask_of(engines), remote_sem=arrive,
+                                 src=in_, dst=out)
+
+    def lists(q, name, groups):
+        src, to, w = T[name], T[name + "32"], T[name].shape[1]
+        for k in groups:
+            q.dma_start(to[16 * k:16 * k + 16, 0:w], src[0:16, 0:w]).then_inc(sem["l_" + name], 16)
+    Y.dma_start(T.nwt[:, 0:4 * NW], T.nw[:, 0:4 * NW]).then_inc(sem.l_nw, 16)
+    lists(Y, "wr", range(0, 4))
+    lists(S, "wr", range(4, 8))
+    lists(Y, "wp", range(0, 4))
+    lists(S, "wp", range(4, 8))
+    S.dma_start(T.plt[:, :], T.pl[:, :]).then_inc(sem.l_pl, 16)
+    lists(Y, "rd", range(0, 8))
+    lists(Y, "pg", range(0, 8))
+
+    g.iota(T.pi[:, 0:1], [[1, 1]], 0, 1).then_inc(sem.io_c, 1)
+    g.iota(T.ki[:, 0:8], [[16, 8]], 16 * PG, 0).then_inc(sem.io_c, 1)
+    g.iota(T.bi[:, 0:25], [[16, 25]], NSL - 16, 0).then_inc(sem.io_c, 1)
+    g.iota(T.si[:, 0:48], [[16, 48]], 0, 0).then_inc(sem.io_c, 1)
+    g.iota(T.kv[:, 0:NSL], [[1, NSL]], 0, 0, allow_small_or_imprecise_dtypes=True).then_inc(sem.io_c, 1)
+    V.memset(T.nwt[:, 4 * NW:512], 0.0).then_inc(sem.c_nw, 1)
+    V.memset(T.X[:, 0:528], 1024.0).then_inc(sem.c_x, 1)
+    V.wait_ge(sem.io_c, 5)
+    for j, bits in enumerate((15, 31, 16)):
+        V.tensor_scalar(T.pb[:, j:j + 1], T.pi[:, 0:1], bits, None, A.bitwise_and).then_inc(sem.c_b, 1)
+    V.wait_ge(sem.c_b, 3)
+    V.tensor_copy(T.col[:, 0:2], T.pb[:, 0:2]).then_inc(sem.c_c, 1)
+    V.tensor_scalar(T.col[:, 2:3], T.pb[:, 2:3], -1.0, 16.0, A.mult, A.add).then_inc(sem.c_c, 1)
+    V.tensor_scalar(T.col[:, 3:4], T.pb[:, 2:3], -0.0625, 1.0, A.mult, A.add).then_inc(sem.c_c, 1)
+    V.wait_ge(sem.c_c, 3)
+    V.tensor_scalar(T.kk[:, 0:8], T.ki[:, 0:8], T.col[:, 0:1], None, A.add).then_inc(sem.c_d, 1)
+    V.tensor_scalar(T.be[:, 0:25], T.bi[:, 0:25], T.col[:, 1:2], None, A.add).then_inc(sem.c_d, 1)
+    V.tensor_scalar(T.se[:, 0:48], T.si[:, 0:48], T.col[:, 0:1], None, A.add).then_inc(sem.c_d, 1)
+
+    V.wait_ge(sem.c_nw, 1)
+    V.wait_ge(sem.l_nw, 16)
+    V.quantize_mx(T.nwq[:, 0:128], T.nws[:, 0:128], T.nwt[:, 0:512]).then_inc(sem.q_nw, 1)
+    V.wait_ge(sem.l_wr, 128)
+    V.tensor_scalar(T.o1[:, 0:8], T.wr32[:, 0:8], 0.0, None, A.max).then_inc(sem.v_o1, 1)
+    lo, hi = min(dests), max(dests) + 1
+
+    def pick1(out, outs, a, b, oc, cs, ss):
+        w = CW * (b - a)
+        V.tensor_copy(out[:, oc:oc + w].bitcast(dt.uint32), T.nwq[:, 0:NW].bitcast(dt.uint32).indirect(T.o1[:, 2 * a:2 * b])).then_inc(cs, 1)
+        S.activation(outs[:, oc:oc + w], T.nws[:, 0:NW].indirect(T.o1[:, 2 * a:2 * b]), COPY).then_inc(ss, 1)
+    for q in (V, S):
+        q.wait_ge(sem.q_nw, 1)
+        q.wait_ge(sem.v_o1, 1)
+    pick1(T.sl1, T.sl1s, lo, hi, CW * lo, sem.p1c, sem.p1s)
+    pick1(T.win, T.wins, me, me + 1, CW * me, sem.own1c, sem.own1s)
+    at = slice(CW * me, CW * me + CW)
+    g.wait_ge(sem.p1c, 1)
+    g.remote_dma_fused([send(T.win[:, at].bitcast(dt.uint8), T.sl1[:, CW * d:CW * d + CW].bitcast(dt.uint8), d, e1[d], sem.a1c)
+                        for d in dests], local_sem=sem.sent1)
+    g.wait_ge(sem.p1s, 1)
+    g.remote_dma_fused([send(T.wins[:, at], T.sl1s[:, CW * d:CW * d + CW], d, e1[d], sem.a1s) for d in dests], local_sem=sem.sent1)
+    Y.wait_ge(sem.sent1, 2 * sum(len(e) for e in e1.values()))
+    Y.dma_start(T.qwt[:, :], T.qw[:, :]).then_inc(sem.l_qw, 16)
+
+    V.wait_ge(sem.l_wp, 128)
+    V.tensor_scalar(T.t1[:, 0:8], T.wp32[:, 0:8], 1023, None, A.bitwise_and).then_inc(sem.v_t1, 1)
+    V.wait_ge(sem.v_t1, 1)
+    V.wait_ge(sem.c_d, 3)
+    V.tensor_tensor(T.t2[:, 0:8], T.t1[:, 0:8], T.kk[:, 0:8], A.min).then_inc(sem.v_t2, 1)
+    V.wait_ge(sem.v_t2, 1)
+    V.tensor_scalar(T.o2[:, 0:8], T.t2[:, 0:8], T.col[:, 2:3], None, A.add).then_inc(sem.v_o2, 1)
+    V.wait_ge(sem.l_rd, 128)
+    V.tensor_scalar(T.rdo[:, 0:3], T.rd32[:, 0:3], T.col[:, 3:4], 0.0, A.add, A.max).then_inc(sem.v_rdo, 1)
+    V.wait_ge(sem.c_x, 1)
+    V.wait_ge(sem.v_o2, 1)
+    V.tensor_copy(T.X[:, 0:528].indirect(T.o2[:, 0:8]), T.kv[:, 0:NSL]).then_inc(sem.v_x, 1)
+    V.wait_ge(sem.v_x, 1)
+    V.transpose(T.TX[:, 0:416], T.X[:, 0:416]).then_inc(sem.v_tx, 1)
+    V.wait_ge(sem.v_tx, 1)
+    V.tensor_tensor(T.wc[:, 0:25], T.TX[:, 0:400:16], T.be[:, 0:25], A.min).then_inc(sem.v_wc, 1)
+    V.wait_ge(sem.v_wc, 1)
+    V.wait_ge(sem.v_rdo, 1)
+    V.tensor_copy(T.o3[:, 0:48], T.wc[:, 0:25].indirect(T.rdo[:, 0:3])).then_inc(sem.v_o3, 1)
+    V.wait_ge(sem.l_pl, 16)
+    V.quantize_mx(T.win[:, NSL:NSL + 16 * PG], T.wins[:, NSL:NSL + 16 * PG], T.plt[:, 0:64 * PG]).then_inc(sem.q_pl, 1)
+
+    n1 = sum(from1.values())
+    for q, a, o in ((V, sem.a1c, sem.own1c), (S, sem.a1s, sem.own1s)):
+        q.wait_ge(sem.v_o3, 1)
+        q.wait_ge(sem.q_pl, 1)
+        q.wait_ge(o, 1)
+        q.wait_ge(a, n1)
+    for r in dests + [me]:
+        c, k = slice(PC * r, PC * r + PC), slice(CP * r, CP * r + CP)
+        to, tos = (T.land, T.lands) if r == me else (T.sl2, T.sl2s)
+        V.tensor_copy(to[:, c].bitcast(dt.uint32), T.win[:, :].bitcast(dt.uint32).indirect(T.o3[:, k])).then_inc(sem["p2c%d" % r], 1)
+        S.activation(tos[:, c], T.wins[:, :].indirect(T.o3[:, k]), COPY).then_inc(sem["p2s%d" % r], 1)
+    at2 = slice(PC * me, PC * me + PC)
+    sent = 0
+    for ds in (dests[:1], dests[1:]):
+        for d in ds:
+            g.wait_ge(sem["p2c%d" % d], 1)
+        g.remote_dma_fused([send(T.land[:, at2].bitcast(dt.uint8), T.sl2[:, PC * d:PC * d + PC].bitcast(dt.uint8), d, e2[d],
+                                 sem["a2c%d" % me]) for d in ds], local_sem=sem.sent2)
+        for d in ds:
+            g.wait_ge(sem["p2s%d" % d], 1)
+        g.remote_dma_fused([send(T.lands[:, at2], T.sl2s[:, PC * d:PC * d + PC], d, e2[d], sem["a2s%d" % me]) for d in ds],
+                           local_sem=sem.sent2)
+        sent += 2 * sum(len(e2[d]) for d in ds)
+
+    V.wait_ge(sem.l_pg, 128)
+    V.tensor_scalar(T.pgo[:, 0:2], T.pg32[:, 0:2], 0.0, None, A.max).then_inc(sem.v_pgo, 1)
+    V.wait_ge(sem.v_pgo, 1)
+    V.tensor_copy(T.o4[:, 0:SP], T.se[:, 0:48].indirect(T.pgo[:, 0:2])).then_inc(sem.v_o4, 1)
+    V.wait_ge(sem.l_qw, 16)
+    V.quantize_mx(T.qwq[:, 0:128 * O], T.qws[:, 0:128 * O], T.qwt[:, 0:512 * O]).then_inc(sem.q_qw, 1)
+
+    order = [me, dests[0], dests[2], dests[1]]
+    P.wait_ge(sem.q_qw, 1)
+    for q in order:
+        c = slice(PC * q, PC * q + PC)
+        if q == me:
+            P.wait_ge(sem["p2c%d" % q], 1)
+            P.wait_ge(sem["p2s%d" % q], 1)
+        else:
+            P.wait_ge(sem["a2c%d" % q], from2[q])
+            P.wait_ge(sem["a2s%d" % q], from2[q])
+        for o in range(O):
+            b = 512 * (O * q + o)
+            P.matmul_mx(T.ps[:, b:b + PC], T.qwq[:, 128 * o:128 * o + 128], T.qws[:, 128 * o:128 * o + 128],
+                        T.land[:, c], T.lands[:, c], True, True).then_inc(sem["m%d_%d" % (o, q)], 1)
+        b = 512 * O * q
+        V.wait_ge(sem["m0_%d" % q], 1)
+        V.tensor_copy(T.r0[:, c], T.ps[:, b:b + PC]).then_inc(sem["k0_%d" % q], 1)
+        S.wait_ge(sem["m1_%d" % q], 1)
+        S.activation(T.r1[:, c], T.ps[:, b + 512:b + 512 + PC], COPY).then_inc(sem["k1_%d" % q], 1)
+
+    for o, v in ((0, 20), (1, 16)):
+        r, y = (T.r0, T.y0) if o == 0 else (T.r1, T.y1)
+        for q in (V, S):
+            if o == 0:
+                q.wait_ge(sem.v_o4, 1)
+            for k in range(N):
+                q.wait_ge(sem["k%d_%d" % (o, k)], 1)
+        V.tensor_copy(y[:, 0:16 * v], r[:, :].indirect(T.o4[:, 0:v])).then_inc(sem["f%dv" % o], 1)
+        S.activation(y[:, 16 * v:512], r[:, :].indirect(T.o4[:, v:SP]), COPY).then_inc(sem["f%ds" % o], 1)
+        Y.wait_ge(sem["f%dv" % o], 1)
+        Y.wait_ge(sem["f%ds" % o], 1)
+        Y.dma_start(T.y[:, 512 * o:512 * o + 512], y[:, :]).then_inc(sem.stored, 16)
+    Y.wait_ge(sem.stored, 32)
+    g.wait_ge(sem.sent2, sent)

@@ -17,20 +17,21 @@ SCRATCH = {
     "rd32": ("sbuf", [128, 3], "int32"), "pg32": ("sbuf", [128, 2], "int32"),
     "o1": ("sbuf", [128, 8], "uint16"), "o2": ("sbuf", [128, 8], "uint16"), "rdo": ("sbuf", [128, 4], "uint16"),
     "o3": ("sbuf", [128, 48], "uint16"), "pgo": ("sbuf", [128, 2], "uint16"), "o4": ("sbuf", [128, 32], "uint16"),
-    "pi": ("sbuf", [128, 1], "int32"), "pb": ("sbuf", [128, 4], "int32"), "col": ("sbuf", [128, 4], "float32"),
-    "kv": ("sbuf", [128, NSL], "bfloat16"), "ki": ("sbuf", [128, 8], "int32"), "kk": ("sbuf", [128, 8], "int32"),
+    "pi": ("sbuf", [128, 1], "int32"), "p31": ("sbuf", [128, 1], "int32"), "p16": ("sbuf", [128, 1], "int32"),
+    "p15": ("sbuf", [128, 1], "int32"), "col": ("sbuf", [128, 4], "float32"),
+    "kv": ("sbuf", [128, NSL], "bfloat16"), "ki": ("sbuf", [128, 8], "int32"),
     "bi": ("sbuf", [128, 25], "int32"), "be": ("sbuf", [128, 25], "float32"),
     "si": ("sbuf", [128, 48], "int32"), "se": ("sbuf", [128, 48], "float32"),
     "t1": ("sbuf", [128, 8], "int32"), "t2": ("sbuf", [128, 8], "int32"),
-    "X": ("sbuf", [128, 528], "bfloat16"), "TX": ("sbuf", [128, 416], "bfloat16"), "wc": ("sbuf", [128, 25], "float32"),
+    "X": ("sbuf", [128, 640], "bfloat16"), "TX": ("sbuf", [128, 416], "bfloat16"), "wc": ("sbuf", [128, 25], "float32"),
     "ps": ("psum", [128, 512 * N * O], "float32"),
     "r0": ("sbuf", [128, N * PC], "float32"), "r1": ("sbuf", [128, N * PC], "float32"),
     "y0": ("sbuf", [128, 512], "float32"), "y1": ("sbuf", [128, 512], "float32"),
 }
 SEMAPHORES = (["l_nw", "l_wr", "l_wp", "l_rd", "l_pg", "l_pl", "l_qw", "stored"]
-              + ["io_c", "c_nw", "c_x", "c_b", "c_c", "c_d", "q_nw", "q_pl", "q_qw", "v_o1", "v_t1", "v_t2", "v_o2", "v_x", "v_tx",
-                 "v_wc", "v_rdo", "v_o3", "v_pgo", "v_o4"]
-              + ["p1c", "p1s", "own1c", "own1s", "a1c", "a1s", "sent1", "sent2"]
+              + ["i_pi", "i_ki", "i_bi", "i_kv", "i_si", "c_nw", "c_x", "c_b", "c_c", "c_p31", "c_be", "c_p15", "c_col0", "c_se",
+                 "q_nw", "q_pl", "q_qw", "v_o1", "v_t1", "v_t2", "v_o2", "v_x", "v_tx", "v_be", "v_wc", "v_rdo", "v_o3", "v_pgo", "v_o4"]
+              + ["p1c", "p1s", "near1c", "near1s", "own1c", "own1s", "a1c", "a1s", "sent"]
               + [n + str(r) for n in ("p2c", "p2s", "a2c", "a2s", "m0_", "m1_", "k0_", "k1_") for r in range(N)]
               + ["f0v", "f0s", "f1v", "f1s"])
 
@@ -42,10 +43,10 @@ def plan(src, cores, topo):
     near = [c for c in others if c not in off]
     out_eng = topo.engines(src, off[0])
     k = len(off)
-    p = [(c, True, out_eng[j::k], out_eng) for j, c in enumerate(off)]
+    p = [(c, out_eng[j::k], out_eng) for j, c in enumerate(off)]
     for c in near:
         e = [x for x in topo.engines(src, c) if x not in out_eng]
-        p.append((c, False, e[::2], e))
+        p.append((c, e, e))
     return p
 
 
@@ -60,135 +61,160 @@ def rank_program(g, core, T, topo):
     V, S, P, Y, sem = g.vector, g.scalar, g.tensor, g.sync, T.sem
     A, COPY = AluOpType, ActivationFunctionType.Copy
     my = plan(core, T.cores, topo)
-    dests = [T.rank_of(c) for c, _, _, _ in my]
-    where = {T.rank_of(c): topo.addr(c, core) for c, _, _, _ in my}
-    e1 = {T.rank_of(c): e for c, _, e, _ in my}
-    e2 = {T.rank_of(c): e for c, _, _, e in my}
+    dests = [T.rank_of(c) for c, _, _ in my]
+    far, same, near = dests
+    where = {T.rank_of(c): topo.addr(c, core) for c, _, _ in my}
+    e1 = {T.rank_of(c): e for c, e, _ in my}
+    e2 = {T.rank_of(c): e for c, _, e in my}
     from1, from2 = {}, {}
     for s in range(N):
         if s != me:
-            for c, _, a, b in plan(T.cores[s], T.cores, topo):
+            for c, a, b in plan(T.cores[s], T.cores, topo):
                 if c == core:
                     from1[s], from2[s] = len(a), len(b)
+    sent = [0]
 
-    def send(out, in_, d, engines, arrive):
-        rid, pid = where[d]
-        return RemoteDMATransfer(dst_ids=[DstId(rid=rid, pnc=pid)], dma_engine_mask=mask_of(engines), remote_sem=arrive,
-                                 src=in_, dst=out)
+    def send(parts, arrive):
+        ts = []
+        for out, in_, d, e in parts:
+            rid, pid = where[d]
+            ts.append(RemoteDMATransfer(dst_ids=[DstId(rid=rid, pnc=pid)], dma_engine_mask=mask_of(e), remote_sem=arrive,
+                                        src=in_, dst=out))
+            sent[0] += len(e)
+        g.remote_dma_fused(ts, local_sem=sem.sent)
 
-    def lists(q, name, groups):
+    def lists(name):
         src, to, w = T[name], T[name + "32"], T[name].shape[1]
-        for k in groups:
-            q.dma_start(to[16 * k:16 * k + 16, 0:w], src[0:16, 0:w]).then_inc(sem["l_" + name], 16)
+        for k in range(8):
+            (Y, S)[k % 2].dma_start(to[16 * k:16 * k + 16, 0:w], src[0:16, 0:w]).then_inc(sem["l_" + name], 16)
     Y.dma_start(T.nwt[:, 0:4 * NW], T.nw[:, 0:4 * NW]).then_inc(sem.l_nw, 16)
-    lists(Y, "wr", range(0, 4))
-    lists(S, "wr", range(4, 8))
-    lists(Y, "wp", range(0, 4))
-    lists(S, "wp", range(4, 8))
+    lists("wr")
+    lists("wp")
+    lists("rd")
     S.dma_start(T.plt[:, :], T.pl[:, :]).then_inc(sem.l_pl, 16)
-    lists(Y, "rd", range(0, 8))
-    lists(Y, "pg", range(0, 8))
+    Y.wait_ge(sem.v_tx, 1)
+    Y.dma_start(T.qwt[:, :], T.qw[:, :]).then_inc(sem.l_qw, 16)
+    for k in range(8):
+        Y.dma_start(T.pg32[16 * k:16 * k + 16, 0:2], T.pg[0:16, 0:2]).then_inc(sem.l_pg, 16)
 
-    g.iota(T.pi[:, 0:1], [[1, 1]], 0, 1).then_inc(sem.io_c, 1)
-    g.iota(T.ki[:, 0:8], [[16, 8]], 16 * PG, 0).then_inc(sem.io_c, 1)
-    g.iota(T.bi[:, 0:25], [[16, 25]], NSL - 16, 0).then_inc(sem.io_c, 1)
-    g.iota(T.si[:, 0:48], [[16, 48]], 0, 0).then_inc(sem.io_c, 1)
-    g.iota(T.kv[:, 0:NSL], [[1, NSL]], 0, 0, allow_small_or_imprecise_dtypes=True).then_inc(sem.io_c, 1)
+    g.iota(T.pi[:, 0:1], [[1, 1]], 0, 1).then_inc(sem.i_pi, 1)
+    g.iota(T.bi[:, 0:25], [[16, 25]], NSL - 16, 0).then_inc(sem.i_bi, 1)
+    g.iota(T.ki[:, 0:8], [[16, 8]], 16 * PG, 1).then_inc(sem.i_ki, 1)
+    g.iota(T.kv[:, 0:NSL], [[1, NSL]], 0, 0, allow_small_or_imprecise_dtypes=True).then_inc(sem.i_kv, 1)
+    g.iota(T.si[:, 0:48], [[16, 48]], 0, 0).then_inc(sem.i_si, 1)
     V.memset(T.nwt[:, 4 * NW:512], 0.0).then_inc(sem.c_nw, 1)
-    V.memset(T.X[:, 0:528], 1024.0).then_inc(sem.c_x, 1)
-    V.wait_ge(sem.io_c, 5)
-    for j, bits in enumerate((15, 31, 16)):
-        V.tensor_scalar(T.pb[:, j:j + 1], T.pi[:, 0:1], bits, None, A.bitwise_and).then_inc(sem.c_b, 1)
-    V.wait_ge(sem.c_b, 3)
-    V.tensor_copy(T.col[:, 0:2], T.pb[:, 0:2]).then_inc(sem.c_c, 1)
-    V.tensor_scalar(T.col[:, 2:3], T.pb[:, 2:3], -1.0, 16.0, A.mult, A.add).then_inc(sem.c_c, 1)
-    V.tensor_scalar(T.col[:, 3:4], T.pb[:, 2:3], -0.0625, 1.0, A.mult, A.add).then_inc(sem.c_c, 1)
-    V.wait_ge(sem.c_c, 3)
-    V.tensor_scalar(T.kk[:, 0:8], T.ki[:, 0:8], T.col[:, 0:1], None, A.add).then_inc(sem.c_d, 1)
-    V.tensor_scalar(T.be[:, 0:25], T.bi[:, 0:25], T.col[:, 1:2], None, A.add).then_inc(sem.c_d, 1)
-    V.tensor_scalar(T.se[:, 0:48], T.si[:, 0:48], T.col[:, 0:1], None, A.add).then_inc(sem.c_d, 1)
+    V.wait_ge(sem.i_pi, 1)
+    V.tensor_scalar(T.p16[:, 0:1], T.pi[:, 0:1], 16, None, A.bitwise_and).then_inc(sem.c_b, 1)
+    V.tensor_scalar(T.p31[:, 0:1], T.pi[:, 0:1], 31, None, A.bitwise_and).then_inc(sem.c_p31, 1)
+    V.memset(T.X[:, 0:640], 1024.0).then_inc(sem.c_x, 1)
+    V.wait_ge(sem.c_b, 1)
+    V.tensor_scalar(T.col[:, 2:3], T.p16[:, 0:1], -1.0, 16.0, A.mult, A.add).then_inc(sem.c_c, 1)
+    V.tensor_scalar(T.col[:, 3:4], T.p16[:, 0:1], -0.0625, 1.0, A.mult, A.add).then_inc(sem.c_c, 1)
+    V.wait_ge(sem.c_p31, 1)
+    V.tensor_copy(T.col[:, 1:2], T.p31[:, 0:1]).then_inc(sem.c_be, 1)
 
     V.wait_ge(sem.c_nw, 1)
     V.wait_ge(sem.l_nw, 16)
     V.quantize_mx(T.nwq[:, 0:128], T.nws[:, 0:128], T.nwt[:, 0:512]).then_inc(sem.q_nw, 1)
     V.wait_ge(sem.l_wr, 128)
     V.tensor_scalar(T.o1[:, 0:8], T.wr32[:, 0:8], 0.0, None, A.max).then_inc(sem.v_o1, 1)
-    lo, hi = min(dests), max(dests) + 1
 
-    def pick1(out, outs, a, b, oc, cs, ss):
-        w = CW * (b - a)
-        V.tensor_copy(out[:, oc:oc + w].bitcast(dt.uint32), T.nwq[:, 0:NW].bitcast(dt.uint32).indirect(T.o1[:, 2 * a:2 * b])).then_inc(cs, 1)
-        S.activation(outs[:, oc:oc + w], T.nws[:, 0:NW].indirect(T.o1[:, 2 * a:2 * b]), COPY).then_inc(ss, 1)
+    def pick1(out, outs, ranks, cs, ss):
+        a, b = min(ranks), max(ranks) + 1
+        c = slice(CW * a, CW * b)
+        V.tensor_copy(out[:, c].bitcast(dt.uint32), T.nwq[:, 0:NW].bitcast(dt.uint32).indirect(T.o1[:, 2 * a:2 * b])).then_inc(cs, 1)
+        S.activation(outs[:, c], T.nws[:, 0:NW].indirect(T.o1[:, 2 * a:2 * b]), COPY).then_inc(ss, 1)
     for q in (V, S):
         q.wait_ge(sem.q_nw, 1)
         q.wait_ge(sem.v_o1, 1)
-    pick1(T.sl1, T.sl1s, lo, hi, CW * lo, sem.p1c, sem.p1s)
-    pick1(T.win, T.wins, me, me + 1, CW * me, sem.own1c, sem.own1s)
+    pick1(T.sl1, T.sl1s, (far, same), sem.p1c, sem.p1s)
+    pick1(T.sl1, T.sl1s, (near,), sem.near1c, sem.near1s)
     at = slice(CW * me, CW * me + CW)
+
+    def codes1(*ds):
+        send([(T.win[:, at].bitcast(dt.uint8), T.sl1[:, CW * d:CW * d + CW].bitcast(dt.uint8), d, e1[d]) for d in ds], sem.a1c)
     g.wait_ge(sem.p1c, 1)
-    g.remote_dma_fused([send(T.win[:, at].bitcast(dt.uint8), T.sl1[:, CW * d:CW * d + CW].bitcast(dt.uint8), d, e1[d], sem.a1c)
-                        for d in dests], local_sem=sem.sent1)
+    codes1(far, same)
+    g.wait_ge(sem.near1c, 1)
+    codes1(near)
     g.wait_ge(sem.p1s, 1)
-    g.remote_dma_fused([send(T.wins[:, at], T.sl1s[:, CW * d:CW * d + CW], d, e1[d], sem.a1s) for d in dests], local_sem=sem.sent1)
-    Y.wait_ge(sem.sent1, 2 * sum(len(e) for e in e1.values()))
-    Y.dma_start(T.qwt[:, :], T.qw[:, :]).then_inc(sem.l_qw, 16)
+    g.wait_ge(sem.near1s, 1)
+    send([(T.wins[:, at], T.sl1s[:, CW * d:CW * d + CW], d, e1[d]) for d in dests], sem.a1s)
 
     V.wait_ge(sem.l_wp, 128)
     V.tensor_scalar(T.t1[:, 0:8], T.wp32[:, 0:8], 1023, None, A.bitwise_and).then_inc(sem.v_t1, 1)
+    V.wait_ge(sem.i_bi, 1)
+    V.wait_ge(sem.c_be, 1)
+    V.tensor_scalar(T.be[:, 0:25], T.bi[:, 0:25], T.col[:, 1:2], None, A.add).then_inc(sem.v_be, 1)
+    V.wait_ge(sem.i_ki, 1)
     V.wait_ge(sem.v_t1, 1)
-    V.wait_ge(sem.c_d, 3)
-    V.tensor_tensor(T.t2[:, 0:8], T.t1[:, 0:8], T.kk[:, 0:8], A.min).then_inc(sem.v_t2, 1)
+    V.tensor_tensor(T.t2[:, 0:8], T.t1[:, 0:8], T.ki[:, 0:8], A.min).then_inc(sem.v_t2, 1)
+    V.wait_ge(sem.l_rd, 128)
+    V.wait_ge(sem.c_c, 2)
+    V.tensor_scalar(T.rdo[:, 0:3], T.rd32[:, 0:3], T.col[:, 3:4], 0.0, A.add, A.max).then_inc(sem.v_rdo, 1)
     V.wait_ge(sem.v_t2, 1)
     V.tensor_scalar(T.o2[:, 0:8], T.t2[:, 0:8], T.col[:, 2:3], None, A.add).then_inc(sem.v_o2, 1)
-    V.wait_ge(sem.l_rd, 128)
-    V.tensor_scalar(T.rdo[:, 0:3], T.rd32[:, 0:3], T.col[:, 3:4], 0.0, A.add, A.max).then_inc(sem.v_rdo, 1)
     V.wait_ge(sem.c_x, 1)
+    V.wait_ge(sem.i_kv, 1)
     V.wait_ge(sem.v_o2, 1)
-    V.tensor_copy(T.X[:, 0:528].indirect(T.o2[:, 0:8]), T.kv[:, 0:NSL]).then_inc(sem.v_x, 1)
+    V.tensor_copy(T.X[:, 0:640].indirect(T.o2[:, 0:8]), T.kv[:, 0:NSL]).then_inc(sem.v_x, 1)
+    pick1(T.win, T.wins, (me,), sem.own1c, sem.own1s)
     V.wait_ge(sem.v_x, 1)
     V.transpose(T.TX[:, 0:416], T.X[:, 0:416]).then_inc(sem.v_tx, 1)
+    V.wait_ge(sem.v_be, 1)
     V.wait_ge(sem.v_tx, 1)
     V.tensor_tensor(T.wc[:, 0:25], T.TX[:, 0:400:16], T.be[:, 0:25], A.min).then_inc(sem.v_wc, 1)
+    V.wait_ge(sem.l_pl, 16)
+    V.quantize_mx(T.win[:, NSL:NSL + 16 * PG], T.wins[:, NSL:NSL + 16 * PG], T.plt[:, 0:64 * PG]).then_inc(sem.q_pl, 1)
     V.wait_ge(sem.v_wc, 1)
     V.wait_ge(sem.v_rdo, 1)
     V.tensor_copy(T.o3[:, 0:48], T.wc[:, 0:25].indirect(T.rdo[:, 0:3])).then_inc(sem.v_o3, 1)
-    V.wait_ge(sem.l_pl, 16)
-    V.quantize_mx(T.win[:, NSL:NSL + 16 * PG], T.wins[:, NSL:NSL + 16 * PG], T.plt[:, 0:64 * PG]).then_inc(sem.q_pl, 1)
 
     n1 = sum(from1.values())
     for q, a, o in ((V, sem.a1c, sem.own1c), (S, sem.a1s, sem.own1s)):
-        q.wait_ge(sem.v_o3, 1)
-        q.wait_ge(sem.q_pl, 1)
         q.wait_ge(o, 1)
+        q.wait_ge(sem.q_pl, 1)
+        q.wait_ge(sem.v_o3, 1)
         q.wait_ge(a, n1)
-    for r in dests + [me]:
+    for r in (far, near, same, me):
         c, k = slice(PC * r, PC * r + PC), slice(CP * r, CP * r + CP)
         to, tos = (T.land, T.lands) if r == me else (T.sl2, T.sl2s)
         V.tensor_copy(to[:, c].bitcast(dt.uint32), T.win[:, :].bitcast(dt.uint32).indirect(T.o3[:, k])).then_inc(sem["p2c%d" % r], 1)
         S.activation(tos[:, c], T.wins[:, :].indirect(T.o3[:, k]), COPY).then_inc(sem["p2s%d" % r], 1)
     at2 = slice(PC * me, PC * me + PC)
-    sent = 0
-    for ds in (dests[:1], dests[1:]):
+
+    def codes2(*ds):
         for d in ds:
             g.wait_ge(sem["p2c%d" % d], 1)
-        g.remote_dma_fused([send(T.land[:, at2].bitcast(dt.uint8), T.sl2[:, PC * d:PC * d + PC].bitcast(dt.uint8), d, e2[d],
-                                 sem["a2c%d" % me]) for d in ds], local_sem=sem.sent2)
+        send([(T.land[:, at2].bitcast(dt.uint8), T.sl2[:, PC * d:PC * d + PC].bitcast(dt.uint8), d, e2[d]) for d in ds],
+             sem["a2c%d" % me])
+
+    def scales2(*ds):
         for d in ds:
             g.wait_ge(sem["p2s%d" % d], 1)
-        g.remote_dma_fused([send(T.lands[:, at2], T.sl2s[:, PC * d:PC * d + PC], d, e2[d], sem["a2s%d" % me]) for d in ds],
-                           local_sem=sem.sent2)
-        sent += 2 * sum(len(e2[d]) for d in ds)
+        send([(T.lands[:, at2], T.sl2s[:, PC * d:PC * d + PC], d, e2[d]) for d in ds], sem["a2s%d" % me])
+    codes2(far)
+    codes2(near)
+    scales2(far)
+    codes2(same)
+    scales2(same, near)
 
-    V.wait_ge(sem.l_pg, 128)
-    V.tensor_scalar(T.pgo[:, 0:2], T.pg32[:, 0:2], 0.0, None, A.max).then_inc(sem.v_pgo, 1)
-    V.wait_ge(sem.v_pgo, 1)
-    V.tensor_copy(T.o4[:, 0:SP], T.se[:, 0:48].indirect(T.pgo[:, 0:2])).then_inc(sem.v_o4, 1)
     V.wait_ge(sem.l_qw, 16)
     V.quantize_mx(T.qwq[:, 0:128 * O], T.qws[:, 0:128 * O], T.qwt[:, 0:512 * O]).then_inc(sem.q_qw, 1)
+    V.tensor_scalar(T.p15[:, 0:1], T.pi[:, 0:1], 15, None, A.bitwise_and).then_inc(sem.c_p15, 1)
+    V.wait_ge(sem.l_pg, 128)
+    V.tensor_scalar(T.pgo[:, 0:2], T.pg32[:, 0:2], 0.0, None, A.max).then_inc(sem.v_pgo, 1)
+    V.wait_ge(sem.c_p15, 1)
+    V.tensor_copy(T.col[:, 0:1], T.p15[:, 0:1]).then_inc(sem.c_col0, 1)
+    V.wait_ge(sem.c_col0, 1)
+    V.wait_ge(sem.i_si, 1)
+    V.tensor_scalar(T.se[:, 0:48], T.si[:, 0:48], T.col[:, 0:1], None, A.add).then_inc(sem.c_se, 1)
+    V.wait_ge(sem.v_pgo, 1)
+    V.wait_ge(sem.c_se, 1)
+    V.tensor_copy(T.o4[:, 0:SP], T.se[:, 0:48].indirect(T.pgo[:, 0:2])).then_inc(sem.v_o4, 1)
 
-    order = [me, dests[0], dests[2], dests[1]]
     P.wait_ge(sem.q_qw, 1)
-    for q in order:
+    for q in (me, far, near, same):
         c = slice(PC * q, PC * q + PC)
         if q == me:
             P.wait_ge(sem["p2c%d" % q], 1)
@@ -219,4 +245,4 @@ def rank_program(g, core, T, topo):
         Y.wait_ge(sem["f%ds" % o], 1)
         Y.dma_start(T.y[:, 512 * o:512 * o + 512], y[:, :]).then_inc(sem.stored, 16)
     Y.wait_ge(sem.stored, 32)
-    g.wait_ge(sem.sent2, sent)
+    g.wait_ge(sem.sent, sent[0])

from concourse.bass import DstId, RemoteDMATransfer
from concourse.mybir import dt, AluOpType, ActivationFunctionType

N, PG, NW, SP, CW, CP, O = 4, 24, 64, 32, 32, 12, 2
NSL = N * CW
PC = 16 * CP
F8, U8 = "float8_e4m3fn_x4", "uint8"
SCRATCH = {
    "nwt": ("sbuf", [128, 512], "bfloat16"), "plt": ("sbuf", [128, 64 * PG], "bfloat16"), "qwt": ("sbuf", [128, 512 * O], "bfloat16"),
    "nwq": ("sbuf", [128, 128], F8), "nws": ("sbuf", [128, 128], U8),
    "sl1": ("sbuf", [128, NSL], F8), "sl1s": ("sbuf", [128, NSL], U8),
    "win": ("sbuf", [128, NSL + 16 * PG], F8), "wins": ("sbuf", [128, NSL + 16 * PG], U8),
    "sl2": ("sbuf", [128, N * PC], F8), "sl2s": ("sbuf", [128, N * PC], U8),
    "land": ("sbuf", [128, N * PC], F8), "lands": ("sbuf", [128, N * PC], U8),
    "qwq": ("sbuf", [128, 128 * O], F8), "qws": ("sbuf", [128, 128 * O], U8),
    "wr32": ("sbuf", [128, 8], "int32"), "wp32": ("sbuf", [128, 8], "int32"),
    "rd32": ("sbuf", [128, 3], "int32"), "pg32": ("sbuf", [128, 2], "int32"),
    "o1": ("sbuf", [128, 8], "uint16"), "o2": ("sbuf", [128, 8], "uint16"), "rdo": ("sbuf", [128, 4], "uint16"),
    "o3": ("sbuf", [128, 48], "uint16"), "pgo": ("sbuf", [128, 2], "uint16"), "o4": ("sbuf", [128, 32], "uint16"),
    "pi": ("sbuf", [128, 1], "int32"), "p31": ("sbuf", [128, 1], "int32"), "p16": ("sbuf", [128, 1], "int32"),
    "p15": ("sbuf", [128, 1], "int32"), "col": ("sbuf", [128, 4], "float32"),
    "kv": ("sbuf", [128, NSL], "bfloat16"), "ki": ("sbuf", [128, 8], "int32"),
    "bi": ("sbuf", [128, 25], "int32"), "be": ("sbuf", [128, 25], "float32"),
    "si": ("sbuf", [128, 48], "int32"), "se": ("sbuf", [128, 48], "float32"),
    "t1": ("sbuf", [128, 8], "int32"), "t2": ("sbuf", [128, 8], "int32"),
    "X": ("sbuf", [128, 640], "bfloat16"), "TX": ("sbuf", [128, 416], "bfloat16"), "wc": ("sbuf", [128, 25], "float32"),
    "ps": ("psum", [128, 512 * N * O], "float32"),
    "r0": ("sbuf", [128, N * PC], "float32"), "r1": ("sbuf", [128, N * PC], "float32"),
    "y0": ("sbuf", [128, 512], "float32"), "y1": ("sbuf", [128, 512], "float32"),
}
SEMAPHORES = (["l_nw", "l_wr", "l_wp", "l_rd", "l_pg", "l_pl", "l_qw", "stored"]
              + ["i_pi", "i_ki", "i_bi", "i_kv", "i_si", "c_nw", "c_x", "c_b", "c_c", "c_p31", "c_be", "c_p15", "c_col0", "c_se",
                 "q_nw", "q_pl", "q_qw", "v_o1", "v_t1", "v_t2", "v_o2", "v_x", "v_tx", "v_be", "v_wc", "v_rdo", "v_o3", "v_pgo", "v_o4"]
              + ["p1c", "p1s", "near1c", "near1s", "own1c", "own1s", "a1c", "a1s", "sent"]
              + [n + str(r) for n in ("p2c", "p2s", "a2c", "a2s", "m0_", "m1_", "k0_", "k1_") for r in range(N)]
              + ["f0v", "f0s", "f1v", "f1s"])


def plan(src, cores, topo):
    others = [c for c in cores if c != src]
    off = [c for c in others if c not in topo.cores_of(src)]
    off.sort(key=lambda c: topo.die(c) == topo.die(src))
    near = [c for c in others if c not in off]
    out_eng = topo.engines(src, off[0])
    k = len(off)
    p = [(c, out_eng[j::k], out_eng) for j, c in enumerate(off)]
    for c in near:
        e = [x for x in topo.engines(src, c) if x not in out_eng]
        p.append((c, e, e))
    return p


def mask_of(engines):
    return sum(1 << e for e in engines)


def rank_program(g, core, T, topo):
    me = T.rank_of(core)
    if me is None:
        return
    V, S, P, Y, sem = g.vector, g.scalar, g.tensor, g.sync, T.sem
    A, COPY = AluOpType, ActivationFunctionType.Copy
    my = plan(core, T.cores, topo)
    dests = [T.rank_of(c) for c, _, _ in my]
    far, same, near = dests
    where = {T.rank_of(c): topo.addr(c, core) for c, _, _ in my}
    e1 = {T.rank_of(c): e for c, e, _ in my}
    e2 = {T.rank_of(c): e for c, _, e in my}
    from1, from2 = {}, {}
    for s in range(N):
        if s != me:
            for c, a, b in plan(T.cores[s], T.cores, topo):
                if c == core:
                    from1[s], from2[s] = len(a), len(b)
    sent = [0]

    def send(parts, arrive):
        ts = []
        for out, in_, d, e in parts:
            rid, pid = where[d]
            ts.append(RemoteDMATransfer(dst_ids=[DstId(rid=rid, pnc=pid)], dma_engine_mask=mask_of(e), remote_sem=arrive,
                                        src=in_, dst=out))
            sent[0] += len(e)
        g.remote_dma_fused(ts, local_sem=sem.sent)

    def lists(name):
        src, to, w = T[name], T[name + "32"], T[name].shape[1]
        for k in range(8):
            (Y, S)[k % 2].dma_start(to[16 * k:16 * k + 16, 0:w], src[0:16, 0:w]).then_inc(sem["l_" + name], 16)
    Y.dma_start(T.nwt[:, 0:4 * NW], T.nw[:, 0:4 * NW]).then_inc(sem.l_nw, 16)
    lists("wr")
    lists("wp")
    lists("rd")
    S.dma_start(T.plt[:, :], T.pl[:, :]).then_inc(sem.l_pl, 16)
    Y.wait_ge(sem.v_tx, 1)
    Y.dma_start(T.qwt[:, :], T.qw[:, :]).then_inc(sem.l_qw, 16)
    for k in range(8):
        Y.dma_start(T.pg32[16 * k:16 * k + 16, 0:2], T.pg[0:16, 0:2]).then_inc(sem.l_pg, 16)

    g.iota(T.pi[:, 0:1], [[1, 1]], 0, 1).then_inc(sem.i_pi, 1)
    g.iota(T.bi[:, 0:25], [[16, 25]], NSL - 16, 0).then_inc(sem.i_bi, 1)
    g.iota(T.ki[:, 0:8], [[16, 8]], 16 * PG, 1).then_inc(sem.i_ki, 1)
    g.iota(T.kv[:, 0:NSL], [[1, NSL]], 0, 0, allow_small_or_imprecise_dtypes=True).then_inc(sem.i_kv, 1)
    g.iota(T.si[:, 0:48], [[16, 48]], 0, 0).then_inc(sem.i_si, 1)
    V.memset(T.nwt[:, 4 * NW:512], 0.0).then_inc(sem.c_nw, 1)
    V.wait_ge(sem.i_pi, 1)
    V.tensor_scalar(T.p16[:, 0:1], T.pi[:, 0:1], 16, None, A.bitwise_and).then_inc(sem.c_b, 1)
    V.tensor_scalar(T.p31[:, 0:1], T.pi[:, 0:1], 31, None, A.bitwise_and).then_inc(sem.c_p31, 1)
    V.memset(T.X[:, 0:640], 1024.0).then_inc(sem.c_x, 1)
    V.wait_ge(sem.c_b, 1)
    V.tensor_scalar(T.col[:, 2:3], T.p16[:, 0:1], -1.0, 16.0, A.mult, A.add).then_inc(sem.c_c, 1)
    V.tensor_scalar(T.col[:, 3:4], T.p16[:, 0:1], -0.0625, 1.0, A.mult, A.add).then_inc(sem.c_c, 1)
    V.wait_ge(sem.c_p31, 1)
    V.tensor_copy(T.col[:, 1:2], T.p31[:, 0:1]).then_inc(sem.c_be, 1)

    V.wait_ge(sem.c_nw, 1)
    V.wait_ge(sem.l_nw, 16)
    V.quantize_mx(T.nwq[:, 0:128], T.nws[:, 0:128], T.nwt[:, 0:512]).then_inc(sem.q_nw, 1)
    V.wait_ge(sem.l_wr, 128)
    V.tensor_scalar(T.o1[:, 0:8], T.wr32[:, 0:8], 0.0, None, A.max).then_inc(sem.v_o1, 1)

    def pick1(out, outs, ranks, cs, ss):
        a, b = min(ranks), max(ranks) + 1
        c = slice(CW * a, CW * b)
        V.tensor_copy(out[:, c].bitcast(dt.uint32), T.nwq[:, 0:NW].bitcast(dt.uint32).indirect(T.o1[:, 2 * a:2 * b])).then_inc(cs, 1)
        S.activation(outs[:, c], T.nws[:, 0:NW].indirect(T.o1[:, 2 * a:2 * b]), COPY).then_inc(ss, 1)
    for q in (V, S):
        q.wait_ge(sem.q_nw, 1)
        q.wait_ge(sem.v_o1, 1)
    pick1(T.sl1, T.sl1s, (far, same), sem.p1c, sem.p1s)
    pick1(T.sl1, T.sl1s, (near,), sem.near1c, sem.near1s)
    at = slice(CW * me, CW * me + CW)

    def codes1(*ds):
        send([(T.win[:, at].bitcast(dt.uint8), T.sl1[:, CW * d:CW * d + CW].bitcast(dt.uint8), d, e1[d]) for d in ds], sem.a1c)
    g.wait_ge(sem.p1c, 1)
    codes1(far, same)
    g.wait_ge(sem.near1c, 1)
    codes1(near)
    g.wait_ge(sem.p1s, 1)
    g.wait_ge(sem.near1s, 1)
    send([(T.wins[:, at], T.sl1s[:, CW * d:CW * d + CW], d, e1[d]) for d in dests], sem.a1s)

    V.wait_ge(sem.l_wp, 128)
    V.tensor_scalar(T.t1[:, 0:8], T.wp32[:, 0:8], 1023, None, A.bitwise_and).then_inc(sem.v_t1, 1)
    V.wait_ge(sem.i_bi, 1)
    V.wait_ge(sem.c_be, 1)
    V.tensor_scalar(T.be[:, 0:25], T.bi[:, 0:25], T.col[:, 1:2], None, A.add).then_inc(sem.v_be, 1)
    V.wait_ge(sem.i_ki, 1)
    V.wait_ge(sem.v_t1, 1)
    V.tensor_tensor(T.t2[:, 0:8], T.t1[:, 0:8], T.ki[:, 0:8], A.min).then_inc(sem.v_t2, 1)
    V.wait_ge(sem.l_rd, 128)
    V.wait_ge(sem.c_c, 2)
    V.tensor_scalar(T.rdo[:, 0:3], T.rd32[:, 0:3], T.col[:, 3:4], 0.0, A.add, A.max).then_inc(sem.v_rdo, 1)
    V.wait_ge(sem.v_t2, 1)
    V.tensor_scalar(T.o2[:, 0:8], T.t2[:, 0:8], T.col[:, 2:3], None, A.add).then_inc(sem.v_o2, 1)
    V.wait_ge(sem.c_x, 1)
    V.wait_ge(sem.i_kv, 1)
    V.wait_ge(sem.v_o2, 1)
    V.tensor_copy(T.X[:, 0:640].indirect(T.o2[:, 0:8]), T.kv[:, 0:NSL]).then_inc(sem.v_x, 1)
    pick1(T.win, T.wins, (me,), sem.own1c, sem.own1s)
    V.wait_ge(sem.v_x, 1)
    V.transpose(T.TX[:, 0:416], T.X[:, 0:416]).then_inc(sem.v_tx, 1)
    V.wait_ge(sem.v_be, 1)
    V.wait_ge(sem.v_tx, 1)
    V.tensor_tensor(T.wc[:, 0:25], T.TX[:, 0:400:16], T.be[:, 0:25], A.min).then_inc(sem.v_wc, 1)
    V.wait_ge(sem.l_pl, 16)
    V.quantize_mx(T.win[:, NSL:NSL + 16 * PG], T.wins[:, NSL:NSL + 16 * PG], T.plt[:, 0:64 * PG]).then_inc(sem.q_pl, 1)
    V.wait_ge(sem.v_wc, 1)
    V.wait_ge(sem.v_rdo, 1)
    V.tensor_copy(T.o3[:, 0:48], T.wc[:, 0:25].indirect(T.rdo[:, 0:3])).then_inc(sem.v_o3, 1)

    n1 = sum(from1.values())
    for q, a, o in ((V, sem.a1c, sem.own1c), (S, sem.a1s, sem.own1s)):
        q.wait_ge(o, 1)
        q.wait_ge(sem.q_pl, 1)
        q.wait_ge(sem.v_o3, 1)
        q.wait_ge(a, n1)
    for r in (far, near, same, me):
        c, k = slice(PC * r, PC * r + PC), slice(CP * r, CP * r + CP)
        to, tos = (T.land, T.lands) if r == me else (T.sl2, T.sl2s)
        V.tensor_copy(to[:, c].bitcast(dt.uint32), T.win[:, :].bitcast(dt.uint32).indirect(T.o3[:, k])).then_inc(sem["p2c%d" % r], 1)
        S.activation(tos[:, c], T.wins[:, :].indirect(T.o3[:, k]), COPY).then_inc(sem["p2s%d" % r], 1)
    at2 = slice(PC * me, PC * me + PC)

    def codes2(*ds):
        for d in ds:
            g.wait_ge(sem["p2c%d" % d], 1)
        send([(T.land[:, at2].bitcast(dt.uint8), T.sl2[:, PC * d:PC * d + PC].bitcast(dt.uint8), d, e2[d]) for d in ds],
             sem["a2c%d" % me])

    def scales2(*ds):
        for d in ds:
            g.wait_ge(sem["p2s%d" % d], 1)
        send([(T.lands[:, at2], T.sl2s[:, PC * d:PC * d + PC], d, e2[d]) for d in ds], sem["a2s%d" % me])
    codes2(far)
    codes2(near)
    scales2(far)
    codes2(same)
    scales2(same, near)

    V.wait_ge(sem.l_qw, 16)
    V.quantize_mx(T.qwq[:, 0:128 * O], T.qws[:, 0:128 * O], T.qwt[:, 0:512 * O]).then_inc(sem.q_qw, 1)
    V.tensor_scalar(T.p15[:, 0:1], T.pi[:, 0:1], 15, None, A.bitwise_and).then_inc(sem.c_p15, 1)
    V.wait_ge(sem.l_pg, 128)
    V.tensor_scalar(T.pgo[:, 0:2], T.pg32[:, 0:2], 0.0, None, A.max).then_inc(sem.v_pgo, 1)
    V.wait_ge(sem.c_p15, 1)
    V.tensor_copy(T.col[:, 0:1], T.p15[:, 0:1]).then_inc(sem.c_col0, 1)
    V.wait_ge(sem.c_col0, 1)
    V.wait_ge(sem.i_si, 1)
    V.tensor_scalar(T.se[:, 0:48], T.si[:, 0:48], T.col[:, 0:1], None, A.add).then_inc(sem.c_se, 1)
    V.wait_ge(sem.v_pgo, 1)
    V.wait_ge(sem.c_se, 1)
    V.tensor_copy(T.o4[:, 0:SP], T.se[:, 0:48].indirect(T.pgo[:, 0:2])).then_inc(sem.v_o4, 1)

    P.wait_ge(sem.q_qw, 1)
    for q in (me, far, near, same):
        c = slice(PC * q, PC * q + PC)
        if q == me:
            P.wait_ge(sem["p2c%d" % q], 1)
            P.wait_ge(sem["p2s%d" % q], 1)
        else:
            P.wait_ge(sem["a2c%d" % q], from2[q])
            P.wait_ge(sem["a2s%d" % q], from2[q])
        for o in range(O):
            b = 512 * (O * q + o)
            P.matmul_mx(T.ps[:, b:b + PC], T.qwq[:, 128 * o:128 * o + 128], T.qws[:, 128 * o:128 * o + 128],
                        T.land[:, c], T.lands[:, c], True, True).then_inc(sem["m%d_%d" % (o, q)], 1)
        b = 512 * O * q
        V.wait_ge(sem["m0_%d" % q], 1)
        V.tensor_copy(T.r0[:, c], T.ps[:, b:b + PC]).then_inc(sem["k0_%d" % q], 1)
        S.wait_ge(sem["m1_%d" % q], 1)
        S.activation(T.r1[:, c], T.ps[:, b + 512:b + 512 + PC], COPY).then_inc(sem["k1_%d" % q], 1)

    for o, v in ((0, 20), (1, 16)):
        r, y = (T.r0, T.y0) if o == 0 else (T.r1, T.y1)
        for q in (V, S):
            if o == 0:
                q.wait_ge(sem.v_o4, 1)
            for k in range(N):
                q.wait_ge(sem["k%d_%d" % (o, k)], 1)
        V.tensor_copy(y[:, 0:16 * v], r[:, :].indirect(T.o4[:, 0:v])).then_inc(sem["f%dv" % o], 1)
        S.activation(y[:, 16 * v:512], r[:, :].indirect(T.o4[:, v:SP]), COPY).then_inc(sem["f%ds" % o], 1)
        Y.wait_ge(sem["f%dv" % o], 1)
        Y.wait_ge(sem["f%ds" % o], 1)
        Y.dma_start(T.y[:, 512 * o:512 * o + 512], y[:, :]).then_inc(sem.stored, 16)
    Y.wait_ge(sem.stored, 32)
    g.wait_ge(sem.sent, sent[0])
